import numpy as np, ml_dtypes
CORES = [25,29,65,69,153,157,193,197]
N = 8
import mx_ref
BF = ml_dtypes.bfloat16
def entries(a):
    return np.ascontiguousarray(a.T).reshape(-1)
def table(e):
    return np.ascontiguousarray(np.reshape(e, (-1, 16)).T).astype(np.int32)
def cols(t, e):
    v = np.concatenate([t.reshape(128, -1, 4), np.zeros((128, 1, 4), BF)], axis=1)
    return np.ascontiguousarray(v[:, e]).reshape(128, -1)
def decode(q):
    o = []
    for b in range(4):
        e = np.zeros((128, 128, 4), np.float32); e[np.arange(128), np.arange(128), b] = 1
        o.append(mx_ref.matmul(mx_ref.quantize(e.reshape(128, 512).astype(BF)), q))
    return np.stack(o, axis=2).reshape(128, -1)
def f(rng, *shape):
    return mx_ref.flush((rng.standard_normal(shape, dtype=np.float32) * np.exp2(rng.integers(-2, 3, shape[:-1] + (1,)))).astype(BF))
def wide(rng, *shape, cols=0):
    v = rng.standard_normal(shape, dtype=np.float32) * np.exp2(rng.integers(-12, 13, shape)).astype(np.float32)
    if cols: v *= np.repeat(np.exp2(rng.integers(-cols, cols + 1, shape[:-2] + (1, shape[-1] // 4))) * (rng.random(shape[:-2] + (1, shape[-1] // 4)) > 0.0625), 4, axis=-1).astype(np.float32)
    return mx_ref.flush(v.astype(BF))
TC, T, CAPP, O = 512, 128, 16, 2
def lists(rng, n, front=False):
    a = np.full((N, N, CAPP), -1)
    b = np.full((N, N, CAPP), -1)
    for s in range(N):
        for d in range(N):
            k = rng.permutation(CAPP)[:n[s, d]]
            a[s, d, k] = rng.integers(0, T, len(k)); b[d, s, k] = 0
    for d in range(N):
        used = b[d] == 0; u = int(used.sum())
        b[d][used] = np.arange(u) if front else rng.permutation(TC)[:u]
    return {"snd": np.stack([table(a[s]) for s in range(N)]), "plc": np.stack([table(b[d]) for d in range(N)])}
def tiles(rng):
    return {"kc": f(rng, N, 128, 4 * TC), "x": f(rng, N, 128, 4 * T), "qw": f(rng, N, 128, 512 * O)}
def setup_inputs(rng):
    return {**tiles(rng), **lists(rng, rng.integers(0, CAPP + 1, (N, N)))}
def setup_inputs_full(rng):
    return {**tiles(rng), **lists(rng, np.full((N, N), CAPP))}
def setup_inputs_few(rng):
    n = rng.integers(0, 3, (N, N))
    for d in range(N):
        o = rng.permutation([s for s in range(N) if s != d])
        n[o[0], d] = 0; n[o[1], d] = 1
    n[:, rng.integers(0, N)] = 0
    return {**tiles(rng), **lists(rng, n)}
def setup_inputs_front(rng):
    return {**tiles(rng), **lists(rng, rng.integers(1, CAPP + 1, (N, N)), front=True)}
def setup_inputs_own(rng):
    n = rng.integers(0, 3, (N, N)); n[np.arange(N), np.arange(N)] = CAPP
    return {**tiles(rng), **lists(rng, n)}
def setup_inputs_spread(rng):
    d = setup_inputs(rng); d["x"] = wide(rng, N, 128, 4 * T, cols=8); d["kc"] = wide(rng, N, 128, 4 * TC); return d
def check_inputs(d):
    b = []
    a = np.stack([entries(d["snd"][r]).reshape(N, CAPP) for r in range(N)])
    p = np.stack([entries(d["plc"][r]).reshape(N, CAPP) for r in range(N)])
    if a.min() < -1 or a.max() >= T: b.append("snd")
    if p.min() < -1 or p.max() >= TC: b.append("plc")
    if ((a.transpose(1, 0, 2) == -1) != (p == -1)).any(): b.append("plc is -1 exactly where the slot is empty")
    for r in range(N):
        v = p[r][p[r] != -1].tolist()
        if len(set(v)) != len(v): b.append("plc differs"); break
    return b
def reference(kc, x, qw, snd, plc):
    y = np.zeros((N, 128, O * TC), np.float32)
    for r in range(N):
        sent = np.concatenate([cols(x[s], entries(snd[s])[r * CAPP:(r + 1) * CAPP]) for s in range(N)], axis=1)
        got = decode(mx_ref.quantize(sent)).astype(BF).reshape(128, N * CAPP, 4)
        p = entries(plc[r]); used = p >= 0
        c = kc[r].reshape(128, TC, 4).copy()
        c[:, p[used]] = got[:, used]
        c = mx_ref.quantize(np.ascontiguousarray(c).reshape(128, 4 * TC))
        for o in range(O):
            y[r][:, TC * o:TC * o + TC] = mx_ref.matmul(mx_ref.quantize(np.ascontiguousarray(qw[r][:, 512 * o:512 * o + 512])), c)
    return {"y": y}

from concourse.bass import DstId, RemoteDMATransfer
from concourse.mybir import dt, AluOpType, ActivationFunctionType

COPY = ActivationFunctionType.Copy
TC, TX, CAPP = 512, 128, 16
YW = TC + 240
NEAR0, FAR0, REND = 128, 176, 240

SCRATCH = {
    "xs": ("sbuf", [128, 4 * TX], "bfloat16"),
    "kcs": ("sbuf", [128, 4 * TC], "bfloat16"),
    "qws": ("sbuf", [128, 1024], "bfloat16"),
    "sl": ("sbuf", [128, 8], "int32"),
    "pl": ("sbuf", [128, 8], "int32"),
    "pm": ("sbuf", [128, 8], "int32"),
    "pv": ("sbuf", [128, 8], "int32"),
    "pc": ("sbuf", [128, 8], "int32"),
    "it": ("sbuf", [128, 8], "int32"),
    "so": ("sbuf", [128, 8], "uint16"),
    "po": ("sbuf", [128, 8], "uint16"),
    "on": ("sbuf", [128, 516], "bfloat16"),
    "ew": ("sbuf", [128, 516], "bfloat16"),
    "eq": ("sbuf", [128, 512], "float8_e4m3fn_x4"),
    "ep": ("sbuf", [128, 512], "uint8"),
    "xq": ("sbuf", [128, 128], "float8_e4m3fn_x4"),
    "xp": ("sbuf", [128, 128], "uint8"),
    "xd": ("sbuf", [128, 512], "bfloat16"),
    "hf": ("sbuf", [128, 512], "bfloat16"),
    "hn": ("sbuf", [128, 512], "bfloat16"),
    "fq": ("sbuf", [128, 128], "float8_e4m3fn_x4"),
    "fp": ("sbuf", [128, 128], "uint8"),
    "rq": ("sbuf", [128, REND], "float8_e4m3fn_x4"),
    "rp": ("sbuf", [128, REND], "uint8"),
    "kq": ("sbuf", [128, 512], "float8_e4m3fn_x4"),
    "kp": ("sbuf", [128, 512], "uint8"),
    "wq": ("sbuf", [128, 256], "float8_e4m3fn_x4"),
    "wp": ("sbuf", [128, 256], "uint8"),
    "ra": ("sbuf", [128, 64], "float8_e4m3fn_x4"),
    "rb": ("sbuf", [128, 64], "uint8"),
    "yb0": ("sbuf", [128, YW], "float32"),
    "yb1": ("sbuf", [128, YW], "float32"),
    "nr0": ("sbuf", [128, 64], "float32"),
    "nr1": ("sbuf", [128, 64], "float32"),
    "fr0": ("sbuf", [128, 64], "float32"),
    "fr1": ("sbuf", [128, 64], "float32"),
    "psd": ("psum", [128, 2048], "float32"),
    "psk": ("psum", [128, 1024], "float32"),
}
SEMAPHORES = ["ld_x", "ld_s", "ld_k", "ld_w", "ld_p", "st",
              "v_on", "v_z", "g_e", "g_it", "q_e", "q_x", "q_f", "q_n", "q_w", "q_k",
              "so_f", "so_n", "gfv", "gfs", "gnv", "gns", "p1", "p2", "p3", "p4",
              "mm0", "mm1", "mm2", "mm3", "cd0", "cd1", "cd2", "cd3",
              "mk0", "mk1", "cy0", "cy1", "mn0", "mn1", "mf0", "mf1",
              "cn0", "cn1", "cf0", "cf1", "sn0", "sn1", "sf0", "sf1",
              "near", "far", "rel", "left"]


def bits(engs):
    return sum(1 << e for e in engs)


def runs(order):
    out, i = [], 0
    while i < len(order):
        k = i + 1
        if k < len(order) and order[k] > order[i]:
            step = order[k] - order[i]
            while k < len(order) and order[k] - order[k - 1] == step:
                k += 1
            out.append((i, slice(order[i], order[k - 1] + 1, step), k - i))
        else:
            out.append((i, slice(order[i], order[i] + 1), 1))
        i = k
    return out


def near_of(c, T, topo):
    return [d for d in T.cores if d != c and topo.may_write(c, d)]


def far_of(c, T, topo):
    return [d for d in T.cores if d != c and not topo.may_write(c, d)]


def chip_ranks(c, T, topo):
    return [d for d in T.cores if d in topo.cores_of(c)]


def relays(c, T, topo):
    far = far_of(chip_ranks(c, T, topo)[0], T, topo)
    out = []
    for v in (1, 0):
        ks = [k for k in topo.cores_of(c) if T.rank_of(k) is None and topo.die(k) == v
              and all(topo.may_write(k, d) for d in far)]
        out.append((ks[0], ks[1], [d for d in far if topo.die(d) == v]))
    return out


def transfer(src_core, dst_core, engs, sem, src, dst, topo):
    rid, pid = topo.addr(dst_core, src_core)
    return RemoteDMATransfer(dst_ids=[DstId(rid=rid, pnc=pid)], dma_engine_mask=bits(engs), remote_sem=sem, src=src, dst=dst)


def cod(buf, a, b):
    return buf[:, a:b].bitcast(dt.uint8)


def relay_program(g, core, T, topo):
    mine = chip_ranks(core, T, topo)
    for ck, pk, ds in relays(core, T, topo):
        if core not in (ck, pk):
            continue
        engs = topo.engines(core, ds[0])
        n = len(engs) // len(ds)
        share = len(topo.engines(mine[0], core)) // len(far_of(mine[0], T, topo))
        g.wait_ge(T.sem.rel, share * len(mine) * len(ds))
        ts = []
        for j, d in enumerate(ds):
            a, e = FAR0 + CAPP * far_of(d, T, topo).index(mine[0]), engs[n * j:n * j + n]
            if core == ck:
                ts.append(transfer(core, d, e, T.sem.far, cod(T.ra, 32 * j, 32 * j + 32), cod(T.rq, a, a + 32), topo))
            else:
                ts.append(transfer(core, d, e, T.sem.far, T.rb[:, 32 * j:32 * j + 32], T.rp[:, a:a + 32], topo))
        g.remote_dma_fused(ts, local_sem=T.sem.left)
        g.wait_ge(T.sem.left, n * len(ds))


def rank_program(g, core, T, topo):
    if T.rank_of(core) is None:
        if chip_ranks(core, T, topo):
            relay_program(g, core, T, topo)
        return
    S, V, A, P, Y = T.sem, g.vector, g.scalar, g.tensor, g.sync
    near, mine = near_of(core, T, topo), chip_ranks(core, T, topo)
    rl = relays(core, T, topo)
    send_far = [(d, ck, pk, j) for ck, pk, ds in rl for j, d in enumerate(ds)]
    far_cols = [T.rank_of(d) for d, ck, pk, j in send_far]
    near_cols = [T.rank_of(d) for d in near] + [T.rank_of(core)]
    put = [T.rank_of(core)] + [T.rank_of(d) for d in near] + [T.rank_of(d) for d in far_of(core, T, topo)]
    fruns, nruns, pruns = runs(far_cols), runs(near_cols), runs(put)

    Y.dma_start(T.xs[:], T.x[:]).then_inc(S.ld_x, 16)
    for q in range(4, 8):
        Y.dma_start(T.sl[16 * q:16 * q + 16, :], T.snd[:]).then_inc(S.ld_s, 16)
    Y.dma_start(T.kcs[:], T.kc[:]).then_inc(S.ld_k, 16)
    for q in range(8):
        Y.dma_start(T.pl[16 * q:16 * q + 16, :], T.plc[:]).then_inc(S.ld_p, 16)
    for o in (0, 1):
        Y.wait_ge(S["sf%d" % o], 1)
        Y.dma_start(T.y[:, TC * o:TC * o + TC], T["yb%d" % o][:, 0:TC]).then_inc(S.st, 16)
    Y.wait_ge(S.st, 32)

    g.wait_ge(S.v_on, 1)
    g.affine_select(T.ew[:], T.on[:], [[-1, 516]], AluOpType.is_equal, 0.0, 4, 4).then_inc(S.g_e, 1)
    g.iota(T.it[:], [[CAPP, 8]], TC + 1, 1).then_inc(S.g_it, 1)
    eon = topo.engines(core, rl[0][0])
    n = len(eon) // len(send_far)
    me = mine.index(core)
    g.wait_ge(S.q_f, 1)
    for kind in (0, 1):
        ts = []
        for i, (d, ck, pk, j) in enumerate(send_far):
            a, e = 32 * j + CAPP * me, eon[n * i:n * i + n]
            if kind == 0:
                ts.append(transfer(core, ck, e, S.rel, cod(T.fq, 16 * i, 16 * i + 16), cod(T.ra, a, a + 16), topo))
            else:
                ts.append(transfer(core, pk, e, S.rel, T.fp[:, 16 * i:16 * i + 16], T.rb[:, a:a + 16], topo))
        g.remote_dma_fused(ts, local_sem=S.left)
    sent = 2 * n * len(send_far)
    off = [d for d in near if d not in mine]
    on = [d for d in near if d in mine]
    eoff = topo.engines(core, off[0])
    rest = [e for e in topo.engines(core, on[0]) if e not in eoff]
    n = len(eoff) // len(off)
    use = {d: eoff[n * i:n * i + n] for i, d in enumerate(off)}
    n = len(rest) // len(on)
    use.update({d: rest[n * i:n * i + n] for i, d in enumerate(on)})
    g.wait_ge(S.q_n, 1)
    for kind in (0, 1):
        ts = []
        for i, d in enumerate(near):
            a, b = 64 + 16 * i, NEAR0 + CAPP * near_of(d, T, topo).index(core)
            if kind == 0:
                ts.append(transfer(core, d, use[d], S.near, cod(T.rq, a, a + 16), cod(T.rq, b, b + 16), topo))
            else:
                ts.append(transfer(core, d, use[d], S.near, T.rp[:, a:a + 16], T.rp[:, b:b + 16], topo))
            sent += len(use[d])
        g.remote_dma_fused(ts, local_sem=S.left)
    g.wait_ge(S.left, sent)
    n_near = 2 * sum(len(use[d]) for d in near)
    n_far = 0
    for s in far_of(core, T, topo):
        if chip_ranks(s, T, topo)[0] == s:
            for ck, pk, ds in relays(s, T, topo):
                if core in ds:
                    n_far += 2 * (len(topo.engines(ck, core)) // len(ds))

    V.memset(T.on[:], 1.0).then_inc(S.v_on, 1)
    V.memset(T.hf[:, 256:512], 0.0).then_inc(S.v_z, 1)
    V.memset(T.hn[:, 0:256], 0.0).then_inc(S.v_z, 1)
    V.wait_ge(S.g_e, 1)
    for b in range(4):
        V.quantize_mx(T.eq[:, 128 * b:128 * b + 128], T.ep[:, 128 * b:128 * b + 128], T.ew[:, 4 - b:516 - b]).then_inc(S.q_e, 1)
    V.wait_ge(S.ld_x, 16)
    V.quantize_mx(T.xq[:], T.xp[:], T.xs[:]).then_inc(S.q_x, 1)
    V.wait_ge(S.ld_s, 128)
    for i, sl, k in fruns:
        V.tensor_copy(T.so[:, i:i + k], T.sl[:, sl]).then_inc(S.so_f, 1)
    for b in (0, 1):
        V.wait_ge(S["mm%d" % b], 1)
        V.tensor_copy(T.xd[:, 128 * b:128 * b + 128], T.psd[:, 512 * b:512 * b + 128]).then_inc(S["cd%d" % b], 1)
    V.wait_ge(S.so_f, len(fruns))
    for b in (0, 1):
        V.wait_ge(S["cd%d" % b], 1)
        V.tensor_copy(T.hf[:, b:256:4], T.xd[:, 128 * b:128 * b + 128].indirect(T.so[:, 0:4])).then_inc(S.gfv, 1)
    V.wait_ge(S.v_z, 2)
    V.wait_ge(S.gfv, 2)
    V.wait_ge(S.gfs, 2)
    V.quantize_mx(T.fq[:], T.fp[:], T.hf[:]).then_inc(S.q_f, 1)
    for i, sl, k in nruns:
        V.tensor_copy(T.so[:, 4 + i:4 + i + k], T.sl[:, sl]).then_inc(S.so_n, 1)
    V.wait_ge(S.so_n, len(nruns))
    for b in (0, 1):
        V.tensor_copy(T.hn[:, 256 + b:512:4], T.xd[:, 128 * b:128 * b + 128].indirect(T.so[:, 4:8])).then_inc(S.gnv, 1)
    V.wait_ge(S.gnv, 2)
    V.wait_ge(S.gns, 2)
    V.quantize_mx(T.rq[:, 0:128], T.rp[:, 0:128], T.hn[:]).then_inc(S.q_n, 1)
    V.wait_ge(S.ld_w, 16)
    V.quantize_mx(T.wq[:], T.wp[:], T.qws[:]).then_inc(S.q_w, 1)
    V.wait_ge(S.ld_k, 16)
    V.quantize_mx(T.kq[:], T.kp[:], T.kcs[:]).then_inc(S.q_k, 1)
    V.wait_ge(S.ld_p, 128)
    V.tensor_scalar(T.pm[:], T.pl[:], 0, None, AluOpType.is_lt).then_inc(S.p1, 1)
    V.wait_ge(S.g_it, 1)
    V.wait_ge(S.p1, 1)
    V.tensor_tensor(T.pv[:], T.pm[:], T.it[:], AluOpType.mult).then_inc(S.p2, 1)
    V.wait_ge(S.p2, 1)
    V.tensor_tensor(T.pc[:], T.pl[:], T.pv[:], AluOpType.add).then_inc(S.p3, 1)
    V.wait_ge(S.p3, 1)
    for i, sl, k in pruns:
        V.tensor_copy(T.po[:, i:i + k], T.pc[:, sl]).then_inc(S.p4, 1)
    V.wait_ge(S.mk0, 1)
    V.tensor_copy(T.yb0[:, 0:TC], T.psk[:, 0:512]).then_inc(S.cy0, 1)
    V.wait_ge(S.p4, len(pruns))
    V.wait_ge(S.cy0, 1)
    V.wait_ge(S.cn0, 1)
    V.tensor_copy(T.yb0[:, 0:YW].indirect(T.po[:, 0:4]), T.nr0[:]).then_inc(S.sn0, 1)
    V.wait_ge(S.cy1, 1)
    V.wait_ge(S.cn1, 1)
    V.tensor_copy(T.yb1[:, 0:YW].indirect(T.po[:, 0:4]), T.nr1[:]).then_inc(S.sn1, 1)
    V.wait_ge(S.sn0, 1)
    V.wait_ge(S.sn1, 1)
    for o in (0, 1):
        V.wait_ge(S["cf%d" % o], 1)
        V.tensor_copy(T["yb%d" % o][:, 0:YW].indirect(T.po[:, 4:8]), T["fr%d" % o][:]).then_inc(S["sf%d" % o], 1)

    P.wait_ge(S.q_e, 4)
    P.wait_ge(S.q_x, 1)
    for b in (0, 2, 1, 3):
        P.matmul_mx(T.psd[:, 512 * b:512 * b + 128], T.eq[:, 128 * b:128 * b + 128], T.ep[:, 128 * b:128 * b + 128],
                    T.xq[:], T.xp[:], True, True).then_inc(S["mm%d" % b], 1)
    P.wait_ge(S.q_w, 1)
    P.wait_ge(S.q_k, 1)
    for o in (0, 1):
        P.matmul_mx(T.psk[:, 512 * o:512 * o + 512], T.wq[:, 128 * o:128 * o + 128], T.wp[:, 128 * o:128 * o + 128],
                    T.kq[:], T.kp[:], True, True).then_inc(S["mk%d" % o], 1)
    P.wait_ge(S.q_n, 1)
    for name, sem, count, end, bank in (("mn", S.near, n_near, FAR0, 0), ("mf", S.far, n_far, REND, 2)):
        P.wait_ge(sem, count)
        for o in (0, 1):
            P.matmul_mx(T.psd[:, 512 * (bank + o):512 * (bank + o) + 128], T.wq[:, 128 * o:128 * o + 128],
                        T.wp[:, 128 * o:128 * o + 128], T.rq[:, end - 128:end], T.rp[:, end - 128:end],
                        True, True).then_inc(S["%s%d" % (name, o)], 1)

    for q in range(4):
        A.dma_start(T.sl[16 * q:16 * q + 16, :], T.snd[:]).then_inc(S.ld_s, 16)
    A.dma_start(T.qws[:], T.qw[:]).then_inc(S.ld_w, 16)
    for b in (2, 3):
        A.wait_ge(S["mm%d" % b], 1)
        A.activation(T.xd[:, 128 * b:128 * b + 128], T.psd[:, 512 * b:512 * b + 128], COPY).then_inc(S["cd%d" % b], 1)
    A.wait_ge(S.so_f, len(fruns))
    for b in (2, 3):
        A.wait_ge(S["cd%d" % b], 1)
        A.activation(T.hf[:, b:256:4], T.xd[:, 128 * b:128 * b + 128].indirect(T.so[:, 0:4]), COPY).then_inc(S.gfs, 1)
    A.wait_ge(S.so_n, len(nruns))
    for b in (2, 3):
        A.activation(T.hn[:, 256 + b:512:4], T.xd[:, 128 * b:128 * b + 128].indirect(T.so[:, 4:8]), COPY).then_inc(S.gns, 1)
    A.wait_ge(S.mk1, 1)
    A.activation(T.yb1[:, 0:TC], T.psk[:, 512:1024], COPY).then_inc(S.cy1, 1)
    for name, out, bank in (("n", "nr", 0), ("f", "fr", 2)):
        for o in (0, 1):
            A.wait_ge(S["m%s%d" % (name, o)], 1)
            A.activation(T["%s%d" % (out, o)][:], T.psd[:, 512 * (bank + o) + 64:512 * (bank + o) + 128],
                         COPY).then_inc(S["c%s%d" % (name, o)], 1)
